import numpy as np
import ml_dtypes


def mxq(x, axis, fmt="e4m3"):
    dtype, down = {"e4m3": (ml_dtypes.float8_e4m3fn, 7), "e5m2": (ml_dtypes.float8_e5m2, 14)}[fmt]
    v = np.moveaxis(np.asarray(x, np.float32).astype(ml_dtypes.bfloat16).astype(np.float64), axis, -1)
    blocks = v.reshape(v.shape[:-1] + (-1, 32))
    amax = np.abs(blocks).max(-1, keepdims=True)
    byte = np.maximum(np.where(amax > 0, np.frexp(amax)[1] - 1 + 127, 0) - down, 1)
    scale = np.exp2(byte - 127.0)
    codes = (blocks / scale).astype(np.float32).astype(dtype).astype(np.float64)
    return np.moveaxis((codes * scale).reshape(v.shape), -1, axis)


WIDE = False


def mx_kscale(k):
    if not WIDE:
        return np.ones(k)
    levels = np.array([10, -10, 5, -5, 0])
    if k % 512:
        return np.exp2(np.random.permutation(np.resize(levels, k // 32))).repeat(32)
    a = np.empty((k // 512, 16))
    for p in range(k // 512):
        a[p, :8] = np.random.permutation(np.resize(levels, 8))
        for g in range(8):
            far = levels[np.abs(levels - a[p, g]) >= 10]
            a[p, g + 8] = far[np.random.randint(len(far))]
    return np.exp2(a.ravel()).repeat(32)


def f64(x):
    return np.asarray(x).astype(np.float64)


def striped(idx):
    return np.tile(np.asarray(idx).reshape(-1, 16).T, (8, 1)).astype(np.uint16)


def unstriped(offs):
    return offs[:16].T.reshape(-1).astype(np.int64)


E2M1 = np.array([0.0, 0.5, 1.0, 1.5, 2.0, 3.0, 4.0, 6.0, -0.0, -0.5, -1.0, -1.5, -2.0, -3.0, -4.0, -6.0])


def pack_weight(w, fmt):
    k, n = w.shape
    w = f64(np.asarray(w, np.float32).astype(ml_dtypes.bfloat16)).reshape(k // 32, 32, n)
    amax = np.abs(w).max(1)
    if fmt == "e4m3":
        byte = np.frexp(amax)[1] - 1 + 127 - 7
    else:
        mant, ex = np.frexp(amax / 6.0)
        byte = np.where(mant > 0.5, ex, ex - 1) + 127
    byte = np.clip(np.where(amax > 0, byte, 1), 1, 254)
    scaled = (w * np.exp2(127.0 - byte)[:, None, :]).reshape(k, n).astype(np.float32)
    by_word = np.ascontiguousarray(scaled.reshape(k // 512, 128, 4, n).transpose(0, 1, 3, 2))
    if fmt == "e4m3":
        words = by_word.astype(ml_dtypes.float8_e4m3fn).view(np.uint8)
    else:
        c = by_word.astype(ml_dtypes.float4_e2m1fn).view(np.uint8) & 0xF
        words = (c[..., 0::2] | (c[..., 1::2] << 4)).reshape(k // 512, 128, 2 * n)
    return np.ascontiguousarray(words), np.ascontiguousarray(byte.astype(np.uint8).reshape(k // 512, 16, n))


def unpack_weight(words, scales, fmt):
    g, _, n = scales.shape
    words = np.ascontiguousarray(words).reshape(g, 128, n, -1)
    if fmt == "e4m3":
        vals = words.view(ml_dtypes.float8_e4m3fn).astype(np.float64)
    else:
        nib = np.empty((g, 128, n, 4), np.uint8)
        nib[..., 0::2] = words & 0xF
        nib[..., 1::2] = words >> 4
        vals = E2M1[nib]
    vals = vals * np.repeat(np.exp2(scales.astype(np.float64) - 127.0), 8, axis=1)[..., None]
    return vals.transpose(0, 1, 3, 2).reshape(g * 512, n)


def sigmoid(v):
    return 1.0 / (1.0 + np.exp(-v))


def bf(x):
    return np.asarray(x, np.float32).astype(ml_dtypes.bfloat16)


def planes(Y):
    r, m = Y.shape
    b = f64(bf(Y)).reshape(r // 32, 32, m)
    amax = np.abs(b).max(1)
    byte = np.clip(np.where(amax > 0, np.frexp(amax)[1] - 1 + 127 - 7, 1), 1, 254)
    codes = (b * np.exp2(127.0 - byte)[:, None, :]).reshape(r, m).astype(np.float32).astype(ml_dtypes.float8_e4m3fn).view(np.uint8)
    words = codes.reshape(r // 512, 128, 4, m).transpose(0, 1, 3, 2)
    return np.ascontiguousarray(words), np.ascontiguousarray(byte.astype(np.uint8).reshape(r // 512, 16, m))


K, U, I, T, E = 512, 2048, 512, 1024, 512


def setup_inputs():
    n = np.random.standard_normal
    idx = np.random.permutation(T)[:I]
    idx2 = np.random.permutation(U)[:I]
    fk = mx_kscale(K)
    hidp = pack_weight(n((K, U)) / fk[:, None], "e4m3")
    return {
        "wv": (n((K, E)) * 1 / np.sqrt(K) * fk[:, None]).astype(np.float32),
        "hid_words": hidp[0],
        "hid_scales": hidp[1],
        "store": (n((E, T))).astype(np.float32),
        "rate": (np.random.uniform(0.3, 1.0, (1, I))).astype(np.float32),
        "dnew": (n((E, T))).astype(np.float32),
        "offs": striped(idx),
        "offs2": striped(idx2),
    }


def reference(wv, hid_words, hid_scales, store, rate, dnew, offs, offs2):
    idx = unstriped(offs)
    idx2 = unstriped(offs2)
    hidu = unpack_weight(hid_words, hid_scales, "e4m3")
    wvq = mxq(f64(wv), 0, "e4m3")
    hididx2g = hidu[:, idx2]
    v = wvq.T @ hididx2g
    sg = sigmoid(f64(store)[:, idx])
    dl = f64(dnew)[:, idx] * f64(rate) * (sg * (1.0 - sg) * (v - f64(store)[:, idx]) - sg)
    df = np.zeros((E, T))
    df[:, idx] = dl
    y = f64(dnew) + df
    words, scales = planes(y)
    return y, words, scales

@@ -1,0 +1,205 @@
+from contextlib import ExitStack
+
+import concourse.mybir as mybir
+from concourse.masks import make_identity
+
+K, U, I, T, E = 512, 2048, 512, 1024, 512
+FLOPS = 2 * K * E * I
+
+F32 = mybir.dt.float32
+BF16 = mybir.dt.bfloat16
+I32 = mybir.dt.int32
+U32 = mybir.dt.uint32
+U16 = mybir.dt.uint16
+U8 = mybir.dt.uint8
+FP8X4 = mybir.dt.float8_e4m3fn_x4
+ALU = mybir.AluOpType
+ACT = mybir.ActivationFunctionType
+
+P = 128
+PACK = 4
+BANK = 512
+PE_PLANES = 3
+
+
+def tile_attend_bstoreblend_pl_kernel(tc, wv, hid_words, hid_scales, store, rate, dnew, offs, offs2, out_0, out_1, out_2):
+    nc = tc.nc
+    with ExitStack() as ctx:
+        keep = ctx.enter_context(tc.tile_pool(name="keep", bufs=1))
+        work = ctx.enter_context(tc.tile_pool(name="work", bufs=2))
+        psum = ctx.enter_context(tc.psum_pool(name="psum", bufs=1))
+
+        def held(name, shape, dtype, tag=None):
+            return keep.tile(shape, dtype, name=name, tag=tag or name, align_bytes=64)
+
+        slots = keep.tile([P, I // 16], U16, name="slots")
+        tokens = keep.tile([P, I // 16], U16, name="tokens")
+        wv_half = [held("wv%d" % h, [P, PACK, E // 2], F32) for h in range(2)]
+        hid_w = held("hid_w", [P, U], I32)
+        hid_s = held("hid_s", [P, U], U8)
+        rate_col = held("rate_col", [P, PACK], F32)
+        store_sb = [held("store%d" % j, [P, T], F32) for j in range(PACK)]
+        dnew_sb = [held("dnew%d" % j, [P, T], F32) for j in range(PACK)]
+        df = [held("df%d" % j, [P, T], F32) for j in range(PACK)]
+        y = held("y", [P, PACK, T], F32)
+        ident = held("ident", [P, P], F32)
+        warm = held("warm", [P, 8], F32)
+
+        store_v = store.rearrange("(p j) t -> p j t", j=PACK)
+        dnew_v = dnew.rearrange("(p j) t -> p j t", j=PACK)
+        out_v = out_0.rearrange("(p j) t -> p j t", j=PACK)
+        wv_v = wv.rearrange("(p j) e -> p j e", j=PACK)
+
+        nc.gpsimd.memset(hid_s[:].bitcast(I32), 0)
+        make_identity(nc, ident[:])
+
+        for q in range(4):
+            nc.scalar.dma_start(hid_s[32 * q : 32 * q + 4, :].bitcast(I32), hid_scales[0, 4 * q : 4 * q + 4, :].bitcast(I32))
+        nc.sync.dma_start(wv_half[0][:], wv_v[:, :, 0 : E // 2])
+        nc.sync.dma_start(tokens[:], offs2)
+        nc.sync.dma_start(slots[:], offs)
+        nc.sync.dma_start(rate_col[:], rate.rearrange("o (p c) -> p (o c)", c=PACK))
+        nc.sync.dma_start(wv_half[1][:], wv_v[:, :, E // 2 : E])
+        nc.sync.dma_start(hid_w[:], hid_words[0].rearrange("p n t -> p (n t)").bitcast(I32))
+        nc.sync.dma_start(dnew_sb[0][:], dnew_v[:, 0, :])
+        for j in range(PACK):
+            if j + 1 < PACK:
+                nc.sync.dma_start(dnew_sb[j + 1][:], dnew_v[:, j + 1, :])
+            nc.sync.dma_start(store_sb[j][:], store_v[:, j, :])
+
+        for j in range(PACK):
+            nc.vector.memset(df[j][:], 0.0)
+
+        nc.scalar.activation(warm[:], ident[:, 0:8], ACT.Sigmoid)
+
+        wv_bf = held("wv_bf", [P, PACK, P, PACK], BF16)
+        for h in range(2):
+            m0 = h * (P // 2)
+            nc.vector.tensor_copy(
+                wv_bf[:, :, m0 : m0 + P // 2, :].rearrange("p t m j -> p m t j"),
+                wv_half[h][:].rearrange("p j (m t) -> p m t j", t=PACK),
+            )
+        rate_ps = psum.tile([P, PACK, P], F32, name="rate_ps", tag="turn0")
+        for c in range(PACK):
+            nc.tensor.transpose(rate_ps[:, c, :], rate_col[:, c : c + 1].to_broadcast([P, P]), ident[:])
+        rate_sb = held("rate_sb", [P, I], F32)
+        nc.scalar.copy(rate_sb[:].rearrange("x (p c) -> x p c", c=PACK), rate_ps[:].rearrange("x c p -> x p c"))
+
+        wv_codes = held("wv_codes", [P, E], U32)
+        wv_scales = held("wv_scales", [P, E], U8)
+        nc.vector.quantize_mx(
+            out=wv_codes[:].bitcast(FP8X4), scales=wv_scales[:], in_=wv_bf[:].rearrange("p t m j -> p (t m j)")
+        )
+        hs_g = held("hs_g", [P, I], U8)
+        nc.vector.tensor_copy(hs_g[:], hid_s[:].indirect(tokens[:]))
+        hw_g = held("hw_g", [P, I], U32, "hid_s")
+        nc.vector.tensor_copy(hw_g[:], hid_w[:].bitcast(U32).indirect(tokens[:]))
+
+        v_sb = [held("v%d" % j, [P, I], F32) for j in range(PACK)]
+        sg = [held("sg%d" % j, [P, I], F32) for j in range(PACK)]
+        gr = [held("gr%d" % j, [P, I], F32, "hid_w" if j == 0 else None) for j in range(PACK)]
+        diff = [held("diff%d" % j, [P, I], F32) for j in range(PACK)]
+        t1 = [held("t1_%d" % j, [P, I], F32) for j in range(PACK)]
+        t2 = [held("t2_%d" % j, [P, I], F32) for j in range(PACK)]
+
+        def values(j):
+            v_ps = psum.tile([P, I], F32, name="v_ps", tag="v%d" % (j % 2))
+            cols = slice(j * P, (j + 1) * P)
+            nc.tensor.matmul_mx(
+                out=v_ps[:], lhsT=wv_codes[:, cols].bitcast(FP8X4), lhsT_scale=wv_scales[:, cols],
+                rhs=hw_g[:].bitcast(FP8X4), rhs_scale=hs_g[:], start=True, stop=True,
+            )
+            nc.scalar.copy(v_sb[j][:], v_ps[:])
+            nc.scalar.activation(sg[j][:], store_sb[j][:].indirect(slots[:]), ACT.Sigmoid)
+
+        def grad_rate(j):
+            nc.vector.tensor_tensor(gr[j][:], dnew_sb[j][:].indirect(slots[:]), rate_sb[:], ALU.mult)
+
+        def difference(j):
+            nc.vector.tensor_tensor(diff[j][:], store_sb[j][:].indirect(slots[:]), v_sb[j][:], ALU.subtract)
+
+        def slope(j):
+            nc.vector.scalar_tensor_tensor(t1[j][:], sg[j][:], 1.0, diff[j][:], ALU.subtract, ALU.mult)
+
+        def deriv(j):
+            nc.vector.scalar_tensor_tensor(t2[j][:], t1[j][:], 1.0, sg[j][:], ALU.subtract, ALU.mult)
+
+        def scatter(j):
+            nc.vector.tensor_tensor(df[j][:].indirect(slots[:]), t2[j][:], gr[j][:], ALU.mult)
+
+        def add_on_vector(j, h):
+            cols = slice(h * BANK, (h + 1) * BANK)
+            nc.vector.tensor_tensor(y[:, j, cols], dnew_sb[j][:, cols], df[j][:, cols], ALU.add)
+
+        def add_on_tensor(j):
+            for h in range(2):
+                turned = psum.tile([P, BANK], F32, name="turned", tag="turn%d" % h)
+                for b in range(4):
+                    cols = slice(h * BANK + b * P, h * BANK + (b + 1) * P)
+                    blk = turned[:, b * P : (b + 1) * P]
+                    nc.tensor.matmul(blk, dnew_sb[j][:, cols], ident[:], start=True, stop=False, is_transpose=True)
+                    nc.tensor.matmul(blk, df[j][:, cols], ident[:], start=False, stop=True, is_transpose=True)
+                yt = work.tile([P, BANK], F32, name="yt")
+                nc.scalar.copy(yt[:], turned[:])
+                back = psum.tile([P, BANK], F32, name="back", tag="back%d" % h)
+                for b in range(4):
+                    nc.tensor.transpose(back[:, b * P : (b + 1) * P], yt[:, b * P : (b + 1) * P], ident[:])
+                nc.scalar.copy(y[:, j, h * BANK : (h + 1) * BANK], back[:])
+
+        def add(j):
+            if j < PE_PLANES:
+                add_on_tensor(j)
+            else:
+                nc.vector.tensor_tensor(y[:, j, :], dnew_sb[j][:], df[j][:], ALU.add)
+            nc.sync.dma_start(out_v[:, j, :], y[:, j, :])
+
+        y_bf = held("y_bf", [P, T, PACK], BF16)
+
+        def round_pair(eng, j0, cols):
+            dst = y_bf[:, cols, j0 : j0 + 2]
+            src = y[:, j0 : j0 + 2, cols].rearrange("p j t -> p t j")
+            if eng == "s":
+                nc.scalar.copy(dst, src)
+            else:
+                nc.vector.tensor_copy(dst, src)
+
+        values(0)
+        grad_rate(0)
+        difference(0)
+        for j in range(PACK):
+            nxt = j + 1 < PACK
+            if nxt:
+                values(j + 1)
+            slope(j)
+            if nxt:
+                grad_rate(j + 1)
+            elif j > 0:
+                add(j - 1)
+            deriv(j)
+            if nxt:
+                difference(j + 1)
+            scatter(j)
+            if nxt and j > 0:
+                add(j - 1)
+            if j == 2:
+                round_pair("s", 0, slice(0, T))
+
+        last = PACK - 1
+        y_codes = held("y_codes", [P, T], U32)
+        y_scales = held("y_scales", [P, T], U8)
+        words_v = out_1[0].rearrange("p n t -> p (n t)").bitcast(I32)
+        for h in range(2):
+            cols = slice(h * BANK, (h + 1) * BANK)
+            add_on_vector(last, h)
+            nc.sync.dma_start(out_v[:, last, cols], y[:, last, cols])
+        round_pair("s", 2, slice(0, BANK))
+        round_pair("v", 2, slice(BANK, T))
+        for h in (0, 1):
+            cols = slice(h * BANK, (h + 1) * BANK)
+            nc.vector.quantize_mx(
+                out=y_codes[:, cols].bitcast(FP8X4), scales=y_scales[:, cols],
+                in_=y_bf[:, cols, :].rearrange("p t j -> p (t j)"),
+            )
+            nc.sync.dma_start(words_v[:, cols], y_codes[:, cols].bitcast(I32))
+        for q in range(4):
+            nc.scalar.dma_start(out_2[0, 4 * q : 4 * q + 4, :].bitcast(I32), y_scales[32 * q : 32 * q + 4, :].bitcast(I32))

@@ -34,7 +34,7 @@ def tile_attend_bstoreblend_pl_kernel(tc, wv, hid_words, hid_scales, store, rate
 
         slots = keep.tile([P, I // 16], U16, name="slots")
         tokens = keep.tile([P, I // 16], U16, name="tokens")
-        wv_half = [held("wv%d" % h, [P, PACK, E // 2], F32) for h in range(2)]
+        wv_sb = held("wv_sb", [P, PACK, E], F32)
         hid_w = held("hid_w", [P, U], I32)
         hid_s = held("hid_s", [P, U], U8)
         rate_col = held("rate_col", [P, PACK], F32)
@@ -55,16 +55,13 @@ def tile_attend_bstoreblend_pl_kernel(tc, wv, hid_words, hid_scales, store, rate
 
         for q in range(4):
             nc.scalar.dma_start(hid_s[32 * q : 32 * q + 4, :].bitcast(I32), hid_scales[0, 4 * q : 4 * q + 4, :].bitcast(I32))
-        nc.sync.dma_start(wv_half[0][:], wv_v[:, :, 0 : E // 2])
         nc.sync.dma_start(tokens[:], offs2)
         nc.sync.dma_start(slots[:], offs)
         nc.sync.dma_start(rate_col[:], rate.rearrange("o (p c) -> p (o c)", c=PACK))
-        nc.sync.dma_start(wv_half[1][:], wv_v[:, :, E // 2 : E])
+        nc.sync.dma_start(wv_sb[:], wv_v)
         nc.sync.dma_start(hid_w[:], hid_words[0].rearrange("p n t -> p (n t)").bitcast(I32))
-        nc.sync.dma_start(dnew_sb[0][:], dnew_v[:, 0, :])
         for j in range(PACK):
-            if j + 1 < PACK:
-                nc.sync.dma_start(dnew_sb[j + 1][:], dnew_v[:, j + 1, :])
+            nc.sync.dma_start(dnew_sb[j][:], dnew_v[:, j, :])
             nc.sync.dma_start(store_sb[j][:], store_v[:, j, :])
 
         for j in range(PACK):
@@ -72,38 +69,38 @@ def tile_attend_bstoreblend_pl_kernel(tc, wv, hid_words, hid_scales, store, rate
 
         nc.scalar.activation(warm[:], ident[:, 0:8], ACT.Sigmoid)
 
-        wv_bf = held("wv_bf", [P, PACK, P, PACK], BF16)
-        for h in range(2):
-            m0 = h * (P // 2)
-            nc.vector.tensor_copy(
-                wv_bf[:, :, m0 : m0 + P // 2, :].rearrange("p t m j -> p m t j"),
-                wv_half[h][:].rearrange("p j (m t) -> p m t j", t=PACK),
-            )
         rate_ps = psum.tile([P, PACK, P], F32, name="rate_ps", tag="turn0")
         for c in range(PACK):
             nc.tensor.transpose(rate_ps[:, c, :], rate_col[:, c : c + 1].to_broadcast([P, P]), ident[:])
         rate_sb = held("rate_sb", [P, I], F32)
         nc.scalar.copy(rate_sb[:].rearrange("x (p c) -> x p c", c=PACK), rate_ps[:].rearrange("x c p -> x p c"))
 
-        wv_codes = held("wv_codes", [P, E], U32)
-        wv_scales = held("wv_scales", [P, E], U8)
-        nc.vector.quantize_mx(
-            out=wv_codes[:].bitcast(FP8X4), scales=wv_scales[:], in_=wv_bf[:].rearrange("p t m j -> p (t m j)")
-        )
         hs_g = held("hs_g", [P, I], U8)
         nc.vector.tensor_copy(hs_g[:], hid_s[:].indirect(tokens[:]))
-        hw_g = held("hw_g", [P, I], U32, "hid_s")
+        wv_codes = held("wv_codes", [P, E], U32, "hid_s")
+        wv_scales = held("wv_scales", [P, E], U8)
+        wv_bf = [held("wv_bf0", [P, 2, P, PACK], BF16), held("wv_bf1", [P, 2, P, PACK], BF16)]
+        wv_dealt = wv_sb[:].rearrange("p j (m t) -> p m t j", t=PACK)
+        nc.scalar.copy(wv_bf[0][:].rearrange("p t m j -> p m t j"), wv_dealt[:, :, 0:2, :])
+        nc.vector.tensor_copy(wv_bf[1][:].rearrange("p t m j -> p m t j"), wv_dealt[:, :, 2:4, :])
+        for h in (1, 0):
+            cols = slice(h * (E // 2), (h + 1) * (E // 2))
+            nc.vector.quantize_mx(
+                out=wv_codes[:, cols].bitcast(FP8X4), scales=wv_scales[:, cols],
+                in_=wv_bf[h][:].rearrange("p t m j -> p (t m j)"),
+            )
+        hw_g = held("hw_g", [P, I], U32, "wv_bf0")
         nc.vector.tensor_copy(hw_g[:], hid_w[:].bitcast(U32).indirect(tokens[:]))
 
         v_sb = [held("v%d" % j, [P, I], F32) for j in range(PACK)]
         sg = [held("sg%d" % j, [P, I], F32) for j in range(PACK)]
-        gr = [held("gr%d" % j, [P, I], F32, "hid_w" if j == 0 else None) for j in range(PACK)]
-        diff = [held("diff%d" % j, [P, I], F32) for j in range(PACK)]
+        gr = {}
+        diff = {}
         t1 = [held("t1_%d" % j, [P, I], F32) for j in range(PACK)]
         t2 = [held("t2_%d" % j, [P, I], F32) for j in range(PACK)]
 
         def values(j):
-            v_ps = psum.tile([P, I], F32, name="v_ps", tag="v%d" % (j % 2))
+            v_ps = psum.tile([P, I], F32, name="v_ps", tag="v%d" % j)
             cols = slice(j * P, (j + 1) * P)
             nc.tensor.matmul_mx(
                 out=v_ps[:], lhsT=wv_codes[:, cols].bitcast(FP8X4), lhsT_scale=wv_scales[:, cols],
@@ -113,9 +110,11 @@ def tile_attend_bstoreblend_pl_kernel(tc, wv, hid_words, hid_scales, store, rate
             nc.scalar.activation(sg[j][:], store_sb[j][:].indirect(slots[:]), ACT.Sigmoid)
 
         def grad_rate(j):
+            gr[j] = held("gr%d" % j, [P, I], F32, ("hid_w", "gr1", "gr1", "gr1")[j])
             nc.vector.tensor_tensor(gr[j][:], dnew_sb[j][:].indirect(slots[:]), rate_sb[:], ALU.mult)
 
         def difference(j):
+            diff[j] = held("diff%d" % j, [P, I], F32, ("diff0", "diff1", "hid_w", "t2_1")[j])
             nc.vector.tensor_tensor(diff[j][:], store_sb[j][:].indirect(slots[:]), v_sb[j][:], ALU.subtract)
 
         def slope(j):
@@ -131,26 +130,29 @@ def tile_attend_bstoreblend_pl_kernel(tc, wv, hid_words, hid_scales, store, rate
             cols = slice(h * BANK, (h + 1) * BANK)
             nc.vector.tensor_tensor(y[:, j, cols], dnew_sb[j][:, cols], df[j][:, cols], ALU.add)
 
-        def add_on_tensor(j):
+        turned = {}
+
+        def turn(j, src, first):
             for h in range(2):
-                turned = psum.tile([P, BANK], F32, name="turned", tag="turn%d" % h)
+                if first:
+                    turned[j, h] = psum.tile([P, BANK], F32, name="turned", tag="turn%d" % (2 * (j % 2) + h))
                 for b in range(4):
                     cols = slice(h * BANK + b * P, h * BANK + (b + 1) * P)
-                    blk = turned[:, b * P : (b + 1) * P]
-                    nc.tensor.matmul(blk, dnew_sb[j][:, cols], ident[:], start=True, stop=False, is_transpose=True)
-                    nc.tensor.matmul(blk, df[j][:, cols], ident[:], start=False, stop=True, is_transpose=True)
-                yt = work.tile([P, BANK], F32, name="yt")
-                nc.scalar.copy(yt[:], turned[:])
-                back = psum.tile([P, BANK], F32, name="back", tag="back%d" % h)
-                for b in range(4):
-                    nc.tensor.transpose(back[:, b * P : (b + 1) * P], yt[:, b * P : (b + 1) * P], ident[:])
-                nc.scalar.copy(y[:, j, h * BANK : (h + 1) * BANK], back[:])
+                    nc.tensor.matmul(
+                        turned[j, h][:, b * P : (b + 1) * P], src[:, cols], ident[:],
+                        start=first and b == 0, stop=(not first) and b == 3, is_transpose=True,
+                    )
 
         def add(j):
-            if j < PE_PLANES:
-                add_on_tensor(j)
-            else:
-                nc.vector.tensor_tensor(y[:, j, :], dnew_sb[j][:], df[j][:], ALU.add)
+            turn(j, df[j], False)
+            yt = [work.tile([P, BANK], F32, name="yt") for h in range(2)]
+            for h in range(2):
+                nc.scalar.copy(yt[h][:], turned[j, h][:])
+            for h in range(2):
+                back = psum.tile([P, BANK], F32, name="back", tag="turn%d" % (2 * ((j + 1) % 2) + h))
+                for b in range(4):
+                    nc.tensor.transpose(back[:, b * P : (b + 1) * P], yt[h][:, b * P : (b + 1) * P], ident[:])
+                nc.scalar.copy(y[:, j, h * BANK : (h + 1) * BANK], back[:])
             nc.sync.dma_start(out_v[:, j, :], y[:, j, :])
 
         y_bf = held("y_bf", [P, T, PACK], BF16)
@@ -163,26 +165,35 @@ def tile_attend_bstoreblend_pl_kernel(tc, wv, hid_words, hid_scales, store, rate
             else:
                 nc.vector.tensor_copy(dst, src)
 
-        values(0)
+        for j in range(PACK):
+            values(j)
+        turn(0, dnew_sb[0], True)
         grad_rate(0)
         difference(0)
-        for j in range(PACK):
-            nxt = j + 1 < PACK
-            if nxt:
-                values(j + 1)
-            slope(j)
-            if nxt:
-                grad_rate(j + 1)
-            elif j > 0:
-                add(j - 1)
-            deriv(j)
-            if nxt:
-                difference(j + 1)
-            scatter(j)
-            if nxt and j > 0:
-                add(j - 1)
-            if j == 2:
-                round_pair("s", 0, slice(0, T))
+        grad_rate(1)
+        slope(0)
+        difference(1)
+        deriv(0)
+        slope(1)
+        scatter(0)
+        add(0)
+        turn(1, dnew_sb[1], True)
+        deriv(1)
+        difference(2)
+        scatter(1)
+        add(1)
+        turn(2, dnew_sb[2], True)
+        round_pair("s", 0, slice(0, T))
+        slope(2)
+        grad_rate(2)
+        deriv(2)
+        difference(3)
+        scatter(2)
+        add(2)
+        slope(3)
+        grad_rate(3)
+        deriv(3)
+        scatter(3)
 
         last = PACK - 1
         y_codes = held("y_codes", [P, T], U32)
@@ -194,7 +205,7 @@ def tile_attend_bstoreblend_pl_kernel(tc, wv, hid_words, hid_scales, store, rate
             nc.sync.dma_start(out_v[:, last, cols], y[:, last, cols])
         round_pair("s", 2, slice(0, BANK))
         round_pair("v", 2, slice(BANK, T))
-        for h in (0, 1):
+        for h in (1, 0):
             cols = slice(h * BANK, (h + 1) * BANK)
             nc.vector.quantize_mx(
                 out=y_codes[:, cols].bitcast(FP8X4), scales=y_scales[:, cols],

@@ -58,14 +58,17 @@ def tile_attend_bstoreblend_pl_kernel(tc, wv, hid_words, hid_scales, store, rate
         nc.sync.dma_start(tokens[:], offs2)
         nc.sync.dma_start(slots[:], offs)
         nc.sync.dma_start(rate_col[:], rate.rearrange("o (p c) -> p (o c)", c=PACK))
+        nc.sync.dma_start(dnew_sb[0][:], dnew_v[:, 0, :])
         nc.sync.dma_start(wv_sb[:], wv_v)
         nc.sync.dma_start(hid_w[:], hid_words[0].rearrange("p n t -> p (n t)").bitcast(I32))
-        for j in range(PACK):
-            nc.sync.dma_start(dnew_sb[j][:], dnew_v[:, j, :])
-            nc.sync.dma_start(store_sb[j][:], store_v[:, j, :])
+        for name, j in (("d", 1), ("s", 0), ("s", 1), ("s", 2), ("d", 2), ("s", 3), ("d", 3)):
+            if name == "s":
+                nc.sync.dma_start(store_sb[j][:], store_v[:, j, :])
+            else:
+                nc.sync.dma_start(dnew_sb[j][:], dnew_v[:, j, :])
 
         for j in range(PACK):
-            nc.vector.memset(df[j][:], 0.0)
+            (nc.vector if j < 2 else nc.gpsimd).memset(df[j][:], 0.0)
 
         nc.scalar.activation(warm[:], ident[:, 0:8], ACT.Sigmoid)
 
@@ -75,6 +78,13 @@ def tile_attend_bstoreblend_pl_kernel(tc, wv, hid_words, hid_scales, store, rate
         rate_sb = held("rate_sb", [P, I], F32)
         nc.scalar.copy(rate_sb[:].rearrange("x (p c) -> x p c", c=PACK), rate_ps[:].rearrange("x c p -> x p c"))
 
+        gr = {}
+
+        def grad_rate(j):
+            gr[j] = held("gr%d" % j, [P, I], F32, ("gr0", "hid_w", "gr2", "dl2")[j])
+            nc.vector.tensor_tensor(gr[j][:], dnew_sb[j][:].indirect(slots[:]), rate_sb[:], ALU.mult)
+
+        grad_rate(0)
         hs_g = held("hs_g", [P, I], U8)
         nc.vector.tensor_copy(hs_g[:], hid_s[:].indirect(tokens[:]))
         wv_codes = held("wv_codes", [P, E], U32, "hid_s")
@@ -94,10 +104,12 @@ def tile_attend_bstoreblend_pl_kernel(tc, wv, hid_words, hid_scales, store, rate
 
         v_sb = [held("v%d" % j, [P, I], F32) for j in range(PACK)]
         sg = [held("sg%d" % j, [P, I], F32) for j in range(PACK)]
-        gr = {}
+        sq = [held("sq%d" % j, [P, I], F32) for j in range(PACK)]
+        nslope = held("nslope", [P, I], F32)
         diff = {}
-        t1 = [held("t1_%d" % j, [P, I], F32) for j in range(PACK)]
+        t1 = {}
         t2 = [held("t2_%d" % j, [P, I], F32) for j in range(PACK)]
+        dl = [held("dl%d" % j, [P, I], F32) for j in range(PACK - 1)]
 
         def values(j):
             v_ps = psum.tile([P, I], F32, name="v_ps", tag="v%d" % j)
@@ -107,24 +119,33 @@ def tile_attend_bstoreblend_pl_kernel(tc, wv, hid_words, hid_scales, store, rate
                 rhs=hw_g[:].bitcast(FP8X4), rhs_scale=hs_g[:], start=True, stop=True,
             )
             nc.scalar.copy(v_sb[j][:], v_ps[:])
-            nc.scalar.activation(sg[j][:], store_sb[j][:].indirect(slots[:]), ACT.Sigmoid)
 
-        def grad_rate(j):
-            gr[j] = held("gr%d" % j, [P, I], F32, ("hid_w", "gr1", "gr1", "gr1")[j])
-            nc.vector.tensor_tensor(gr[j][:], dnew_sb[j][:].indirect(slots[:]), rate_sb[:], ALU.mult)
+        def gate(j):
+            nc.scalar.activation(sg[j][:], store_sb[j][:].indirect(slots[:]), ACT.Sigmoid)
+            nc.scalar.activation(sq[j][:], sg[j][:], ACT.Square, bias=-0.5)
 
         def difference(j):
-            diff[j] = held("diff%d" % j, [P, I], F32, ("diff0", "diff1", "hid_w", "t2_1")[j])
+            diff[j] = held("diff%d" % j, [P, I], F32, ("diff0", "diff1", "diff2", "dl1")[j])
             nc.vector.tensor_tensor(diff[j][:], store_sb[j][:].indirect(slots[:]), v_sb[j][:], ALU.subtract)
 
         def slope(j):
-            nc.vector.scalar_tensor_tensor(t1[j][:], sg[j][:], 1.0, diff[j][:], ALU.subtract, ALU.mult)
+            t1[j] = held("t1_%d" % j, [P, I], F32, ("t1_0", "t2_0", "dl0", "t1_3")[j])
+            if j < 3:
+                nc.vector.scalar_tensor_tensor(t1[j][:], sq[j][:], 0.25, diff[j][:], ALU.subtract, ALU.mult)
+            else:
+                nc.gpsimd.tensor_tensor(t1[j][:], nslope[:], diff[j][:], ALU.mult)
 
-        def deriv(j):
-            nc.vector.scalar_tensor_tensor(t2[j][:], t1[j][:], 1.0, sg[j][:], ALU.subtract, ALU.mult)
+        def deriv(j, eng):
+            eng.tensor_tensor(t2[j][:], t1[j][:], sg[j][:], ALU.subtract)
+
+        def product(j, eng):
+            eng.tensor_tensor(dl[j][:], t2[j][:], gr[j][:], ALU.mult)
 
         def scatter(j):
-            nc.vector.tensor_tensor(df[j][:].indirect(slots[:]), t2[j][:], gr[j][:], ALU.mult)
+            if j < 3:
+                nc.vector.tensor_copy(df[j][:].indirect(slots[:]), dl[j][:])
+            else:
+                nc.vector.tensor_tensor(df[j][:].indirect(slots[:]), t2[j][:], gr[j][:], ALU.mult)
 
         def add_on_vector(j, h):
             cols = slice(h * BANK, (h + 1) * BANK)
@@ -153,7 +174,7 @@ def tile_attend_bstoreblend_pl_kernel(tc, wv, hid_words, hid_scales, store, rate
                 for b in range(4):
                     nc.tensor.transpose(back[:, b * P : (b + 1) * P], yt[h][:, b * P : (b + 1) * P], ident[:])
                 nc.scalar.copy(y[:, j, h * BANK : (h + 1) * BANK], back[:])
-            nc.sync.dma_start(out_v[:, j, :], y[:, j, :])
+            nc.scalar.dma_start(out_v[:, j, :], y[:, j, :])
 
         y_bf = held("y_bf", [P, T, PACK], BF16)
 
@@ -165,34 +186,42 @@ def tile_attend_bstoreblend_pl_kernel(tc, wv, hid_words, hid_scales, store, rate
             else:
                 nc.vector.tensor_copy(dst, src)
 
-        for j in range(PACK):
+        values(0)
+        values(1)
+        gate(0)
+        gate(1)
+        for j in (2, 3):
             values(j)
+            gate(j)
+        nc.scalar.activation(nslope[:], sq[3][:], ACT.Identity, bias=-0.25)
         turn(0, dnew_sb[0], True)
-        grad_rate(0)
-        difference(0)
         grad_rate(1)
-        slope(0)
+        difference(0)
         difference(1)
-        deriv(0)
+        slope(0)
+        difference(2)
+        deriv(0, nc.vector)
+        grad_rate(2)
+        product(0, nc.vector)
         slope(1)
         scatter(0)
+        deriv(1, nc.gpsimd)
+        product(1, nc.gpsimd)
         add(0)
         turn(1, dnew_sb[1], True)
-        deriv(1)
-        difference(2)
+        slope(2)
         scatter(1)
+        deriv(2, nc.gpsimd)
+        product(2, nc.gpsimd)
         add(1)
         turn(2, dnew_sb[2], True)
         round_pair("s", 0, slice(0, T))
-        slope(2)
-        grad_rate(2)
-        deriv(2)
         difference(3)
         scatter(2)
-        add(2)
         slope(3)
+        deriv(3, nc.gpsimd)
+        add(2)
         grad_rate(3)
-        deriv(3)
         scatter(3)
 
         last = PACK - 1

@@ -18,8 +18,11 @@ ACT = mybir.ActivationFunctionType
 
 P = 128
 PACK = 4
+LAST = PACK - 1
+QUADRANTS = 4
 BANK = 512
-PE_PLANES = 3
+LIST = 16
+SCALAR_COLS = 384
 
 
 def tile_attend_bstoreblend_pl_kernel(tc, wv, hid_words, hid_scales, store, rate, dnew, offs, offs2, out_0, out_1, out_2):
@@ -29,11 +32,14 @@ def tile_attend_bstoreblend_pl_kernel(tc, wv, hid_words, hid_scales, store, rate
         work = ctx.enter_context(tc.tile_pool(name="work", bufs=2))
         psum = ctx.enter_context(tc.psum_pool(name="psum", bufs=1))
 
-        def held(name, shape, dtype, tag=None):
-            return keep.tile(shape, dtype, name=name, tag=tag or name, align_bytes=64)
+        def held(name, shape, dtype, reuse=None):
+            return keep.tile(shape, dtype, name=name, tag=reuse or name, align_bytes=64)
 
-        slots = keep.tile([P, I // 16], U16, name="slots")
-        tokens = keep.tile([P, I // 16], U16, name="tokens")
+        def slot_tile(name, j, reuse=None):
+            return held("%s%d" % (name, j), [P, I], F32, reuse)
+
+        places = keep.tile([P, I // LIST], U16, name="places")
+        tokens = keep.tile([P, I // LIST], U16, name="tokens")
         wv_sb = held("wv_sb", [P, PACK, E], F32)
         hid_w = held("hid_w", [P, U], I32)
         hid_s = held("hid_s", [P, U], U8)
@@ -43,34 +49,35 @@ def tile_attend_bstoreblend_pl_kernel(tc, wv, hid_words, hid_scales, store, rate
         df = [held("df%d" % j, [P, T], F32) for j in range(PACK)]
         y = held("y", [P, PACK, T], F32)
         ident = held("ident", [P, P], F32)
-        warm = held("warm", [P, 8], F32)
 
-        store_v = store.rearrange("(p j) t -> p j t", j=PACK)
-        dnew_v = dnew.rearrange("(p j) t -> p j t", j=PACK)
-        out_v = out_0.rearrange("(p j) t -> p j t", j=PACK)
-        wv_v = wv.rearrange("(p j) e -> p j e", j=PACK)
+        store_planes = store.rearrange("(p j) t -> p j t", j=PACK)
+        dnew_planes = dnew.rearrange("(p j) t -> p j t", j=PACK)
+        out_planes = out_0.rearrange("(p j) t -> p j t", j=PACK)
 
         nc.gpsimd.memset(hid_s[:].bitcast(I32), 0)
         make_identity(nc, ident[:])
 
-        for q in range(4):
+        for q in range(QUADRANTS):
             nc.scalar.dma_start(hid_s[32 * q : 32 * q + 4, :].bitcast(I32), hid_scales[0, 4 * q : 4 * q + 4, :].bitcast(I32))
         nc.sync.dma_start(tokens[:], offs2)
-        nc.sync.dma_start(slots[:], offs)
+        nc.sync.dma_start(places[:], offs)
         nc.sync.dma_start(rate_col[:], rate.rearrange("o (p c) -> p (o c)", c=PACK))
-        nc.sync.dma_start(dnew_sb[0][:], dnew_v[:, 0, :])
-        nc.sync.dma_start(wv_sb[:], wv_v)
-        nc.sync.dma_start(hid_w[:], hid_words[0].rearrange("p n t -> p (n t)").bitcast(I32))
-        for name, j in (("d", 1), ("s", 0), ("s", 1), ("s", 2), ("d", 2), ("s", 3), ("d", 3)):
-            if name == "s":
-                nc.sync.dma_start(store_sb[j][:], store_v[:, j, :])
-            else:
-                nc.sync.dma_start(dnew_sb[j][:], dnew_v[:, j, :])
+        nc.sync.dma_start(wv_sb[:], wv.rearrange("(p r) e -> p r e", r=PACK))
+        nc.sync.dma_start(dnew_sb[0][:], dnew_planes[:, 0, :])
+        nc.sync.dma_start(hid_w[:], hid_words[0].rearrange("p n r -> p (n r)").bitcast(I32))
+        nc.sync.dma_start(dnew_sb[1][:], dnew_planes[:, 1, :])
+        nc.sync.dma_start(store_sb[0][:], store_planes[:, 0, :])
+        nc.sync.dma_start(store_sb[1][:], store_planes[:, 1, :])
+        nc.sync.dma_start(dnew_sb[2][:], dnew_planes[:, 2, :])
+        nc.sync.dma_start(store_sb[2][:], store_planes[:, 2, :])
+        nc.sync.dma_start(store_sb[3][:], store_planes[:, 3, :])
+        nc.sync.dma_start(dnew_sb[3][:], dnew_planes[:, 3, :])
 
         for j in range(PACK):
-            (nc.vector if j < 2 else nc.gpsimd).memset(df[j][:], 0.0)
+            (nc.vector if j < PACK // 2 else nc.gpsimd).memset(df[j][:], 0.0)
 
-        nc.scalar.activation(warm[:], ident[:, 0:8], ACT.Sigmoid)
+        centre = held("centre", [P, 1], F32)
+        nc.scalar.activation(centre[:], ident[:, 0:1], ACT.Sigmoid, scale=0.0)
 
         rate_ps = psum.tile([P, PACK, P], F32, name="rate_ps", tag="turn0")
         for c in range(PACK):
@@ -78,78 +85,74 @@ def tile_attend_bstoreblend_pl_kernel(tc, wv, hid_words, hid_scales, store, rate
         rate_sb = held("rate_sb", [P, I], F32)
         nc.scalar.copy(rate_sb[:].rearrange("x (p c) -> x p c", c=PACK), rate_ps[:].rearrange("x c p -> x p c"))
 
-        gr = {}
+        grad_rate = {}
 
-        def grad_rate(j):
-            gr[j] = held("gr%d" % j, [P, I], F32, ("gr0", "hid_w", "gr2", "dl2")[j])
-            nc.vector.tensor_tensor(gr[j][:], dnew_sb[j][:].indirect(slots[:]), rate_sb[:], ALU.mult)
+        def gather_grad(j, reuse=None):
+            grad_rate[j] = slot_tile("grad_rate", j, reuse)
+            nc.vector.tensor_tensor(grad_rate[j][:], dnew_sb[j][:].indirect(places[:]), rate_sb[:], ALU.mult)
 
-        grad_rate(0)
-        hs_g = held("hs_g", [P, I], U8)
-        nc.vector.tensor_copy(hs_g[:], hid_s[:].indirect(tokens[:]))
+        gather_grad(0)
+        hid_s_listed = held("hid_s_listed", [P, I], U8)
+        nc.vector.tensor_copy(hid_s_listed[:], hid_s[:].indirect(tokens[:]))
+
         wv_codes = held("wv_codes", [P, E], U32, "hid_s")
         wv_scales = held("wv_scales", [P, E], U8)
-        wv_bf = [held("wv_bf0", [P, 2, P, PACK], BF16), held("wv_bf1", [P, 2, P, PACK], BF16)]
-        wv_dealt = wv_sb[:].rearrange("p j (m t) -> p m t j", t=PACK)
-        nc.scalar.copy(wv_bf[0][:].rearrange("p t m j -> p m t j"), wv_dealt[:, :, 0:2, :])
-        nc.vector.tensor_copy(wv_bf[1][:].rearrange("p t m j -> p m t j"), wv_dealt[:, :, 2:4, :])
+        wv_bf = [held("wv_bf%d" % h, [P, 2, P, PACK], BF16) for h in range(2)]
+        wv_dealt = wv_sb[:].rearrange("p r (m j) -> p m j r", j=PACK)
+        nc.scalar.copy(wv_bf[0][:].rearrange("p j m r -> p m j r"), wv_dealt[:, :, 0:2, :])
+        nc.vector.tensor_copy(wv_bf[1][:].rearrange("p j m r -> p m j r"), wv_dealt[:, :, 2:4, :])
         for h in (1, 0):
             cols = slice(h * (E // 2), (h + 1) * (E // 2))
             nc.vector.quantize_mx(
-                out=wv_codes[:, cols].bitcast(FP8X4), scales=wv_scales[:, cols],
-                in_=wv_bf[h][:].rearrange("p t m j -> p (t m j)"),
+                out=wv_codes[:, cols].bitcast(FP8X4),
+                scales=wv_scales[:, cols],
+                in_=wv_bf[h][:].rearrange("p j m r -> p (j m r)"),
             )
-        hw_g = held("hw_g", [P, I], U32, "wv_bf0")
-        nc.vector.tensor_copy(hw_g[:], hid_w[:].bitcast(U32).indirect(tokens[:]))
+        hid_w_listed = held("hid_w_listed", [P, I], U32, "wv_bf0")
+        nc.vector.tensor_copy(hid_w_listed[:], hid_w[:].bitcast(U32).indirect(tokens[:]))
 
-        v_sb = [held("v%d" % j, [P, I], F32) for j in range(PACK)]
-        sg = [held("sg%d" % j, [P, I], F32) for j in range(PACK)]
-        sq = [held("sq%d" % j, [P, I], F32) for j in range(PACK)]
-        nslope = held("nslope", [P, I], F32)
+        v_sb = [slot_tile("v", j) for j in range(PACK)]
+        sg = [slot_tile("sg", j) for j in range(PACK)]
+        off_sq = {j: slot_tile("off_sq", j) for j in range(1, PACK)}
+        neg_slope = held("neg_slope", [P, I], F32)
+        deriv = [slot_tile("deriv", j) for j in range(PACK)]
+        dl = [slot_tile("dl", j) for j in range(LAST)]
         diff = {}
-        t1 = {}
-        t2 = [held("t2_%d" % j, [P, I], F32) for j in range(PACK)]
-        dl = [held("dl%d" % j, [P, I], F32) for j in range(PACK - 1)]
+        term = {}
 
         def values(j):
             v_ps = psum.tile([P, I], F32, name="v_ps", tag="v%d" % j)
             cols = slice(j * P, (j + 1) * P)
             nc.tensor.matmul_mx(
-                out=v_ps[:], lhsT=wv_codes[:, cols].bitcast(FP8X4), lhsT_scale=wv_scales[:, cols],
-                rhs=hw_g[:].bitcast(FP8X4), rhs_scale=hs_g[:], start=True, stop=True,
+                out=v_ps[:],
+                lhsT=wv_codes[:, cols].bitcast(FP8X4),
+                lhsT_scale=wv_scales[:, cols],
+                rhs=hid_w_listed[:].bitcast(FP8X4),
+                rhs_scale=hid_s_listed[:],
+                start=True,
+                stop=True,
             )
             nc.scalar.copy(v_sb[j][:], v_ps[:])
 
         def gate(j):
-            nc.scalar.activation(sg[j][:], store_sb[j][:].indirect(slots[:]), ACT.Sigmoid)
-            nc.scalar.activation(sq[j][:], sg[j][:], ACT.Square, bias=-0.5)
+            nc.scalar.activation(sg[j][:], store_sb[j][:].indirect(places[:]), ACT.Sigmoid)
+            if j in off_sq:
+                nc.scalar.activation(off_sq[j][:], sg[j][:], ACT.Square, bias=centre[:], scale=-1.0)
 
-        def difference(j):
-            diff[j] = held("diff%d" % j, [P, I], F32, ("diff0", "diff1", "diff2", "dl1")[j])
-            nc.vector.tensor_tensor(diff[j][:], store_sb[j][:].indirect(slots[:]), v_sb[j][:], ALU.subtract)
+        def gather_diff(j, reuse=None):
+            diff[j] = slot_tile("diff", j, reuse)
+            nc.vector.tensor_tensor(diff[j][:], store_sb[j][:].indirect(places[:]), v_sb[j][:], ALU.subtract)
 
-        def slope(j):
-            t1[j] = held("t1_%d" % j, [P, I], F32, ("t1_0", "t2_0", "dl0", "t1_3")[j])
-            if j < 3:
-                nc.vector.scalar_tensor_tensor(t1[j][:], sq[j][:], 0.25, diff[j][:], ALU.subtract, ALU.mult)
-            else:
-                nc.gpsimd.tensor_tensor(t1[j][:], nslope[:], diff[j][:], ALU.mult)
+        def slope_term(j, reuse):
+            term[j] = slot_tile("term", j, reuse)
+            nc.vector.scalar_tensor_tensor(term[j][:], off_sq[j][:], 0.25, diff[j][:], ALU.subtract, ALU.mult)
 
-        def deriv(j, eng):
-            eng.tensor_tensor(t2[j][:], t1[j][:], sg[j][:], ALU.subtract)
-
-        def product(j, eng):
-            eng.tensor_tensor(dl[j][:], t2[j][:], gr[j][:], ALU.mult)
+        def finish_on_gpsimd(j):
+            nc.gpsimd.tensor_tensor(deriv[j][:], term[j][:], sg[j][:], ALU.subtract)
+            nc.gpsimd.tensor_tensor(dl[j][:], deriv[j][:], grad_rate[j][:], ALU.mult)
 
         def scatter(j):
-            if j < 3:
-                nc.vector.tensor_copy(df[j][:].indirect(slots[:]), dl[j][:])
-            else:
-                nc.vector.tensor_tensor(df[j][:].indirect(slots[:]), t2[j][:], gr[j][:], ALU.mult)
-
-        def add_on_vector(j, h):
-            cols = slice(h * BANK, (h + 1) * BANK)
-            nc.vector.tensor_tensor(y[:, j, cols], dnew_sb[j][:, cols], df[j][:, cols], ALU.add)
+            nc.vector.tensor_copy(df[j][:].indirect(places[:]), dl[j][:])
 
         turned = {}
 
@@ -157,89 +160,94 @@ def tile_attend_bstoreblend_pl_kernel(tc, wv, hid_words, hid_scales, store, rate
             for h in range(2):
                 if first:
                     turned[j, h] = psum.tile([P, BANK], F32, name="turned", tag="turn%d" % (2 * (j % 2) + h))
-                for b in range(4):
+                for b in range(BANK // P):
                     cols = slice(h * BANK + b * P, h * BANK + (b + 1) * P)
                     nc.tensor.matmul(
-                        turned[j, h][:, b * P : (b + 1) * P], src[:, cols], ident[:],
-                        start=first and b == 0, stop=(not first) and b == 3, is_transpose=True,
+                        turned[j, h][:, b * P : (b + 1) * P],
+                        src[:, cols],
+                        ident[:],
+                        start=first and b == 0,
+                        stop=(not first) and b == BANK // P - 1,
+                        is_transpose=True,
                     )
 
-        def add(j):
+        def add_on_tensor(j):
             turn(j, df[j], False)
-            yt = [work.tile([P, BANK], F32, name="yt") for h in range(2)]
+            y_turned = [work.tile([P, BANK], F32, name="y_turned") for h in range(2)]
             for h in range(2):
-                nc.scalar.copy(yt[h][:], turned[j, h][:])
+                nc.scalar.copy(y_turned[h][:], turned[j, h][:])
             for h in range(2):
                 back = psum.tile([P, BANK], F32, name="back", tag="turn%d" % (2 * ((j + 1) % 2) + h))
-                for b in range(4):
-                    nc.tensor.transpose(back[:, b * P : (b + 1) * P], yt[h][:, b * P : (b + 1) * P], ident[:])
+                for b in range(BANK // P):
+                    nc.tensor.transpose(back[:, b * P : (b + 1) * P], y_turned[h][:, b * P : (b + 1) * P], ident[:])
                 nc.scalar.copy(y[:, j, h * BANK : (h + 1) * BANK], back[:])
-            nc.scalar.dma_start(out_v[:, j, :], y[:, j, :])
+            nc.scalar.dma_start(out_planes[:, j, :], y[:, j, :])
 
         y_bf = held("y_bf", [P, T, PACK], BF16)
 
-        def round_pair(eng, j0, cols):
-            dst = y_bf[:, cols, j0 : j0 + 2]
-            src = y[:, j0 : j0 + 2, cols].rearrange("p j t -> p t j")
-            if eng == "s":
-                nc.scalar.copy(dst, src)
-            else:
-                nc.vector.tensor_copy(dst, src)
+        def round_pair(copy, j0, cols):
+            copy(y_bf[:, cols, j0 : j0 + 2], y[:, j0 : j0 + 2, cols].rearrange("p j t -> p t j"))
 
         values(0)
         values(1)
         gate(0)
+        values(2)
         gate(1)
-        for j in (2, 3):
-            values(j)
-            gate(j)
-        nc.scalar.activation(nslope[:], sq[3][:], ACT.Identity, bias=-0.25)
+        gate(2)
+        values(LAST)
+        gate(LAST)
+        nc.scalar.activation(neg_slope[:], off_sq[LAST][:], ACT.Identity, bias=-0.25)
         turn(0, dnew_sb[0], True)
-        grad_rate(1)
-        difference(0)
-        difference(1)
-        slope(0)
-        difference(2)
-        deriv(0, nc.vector)
-        grad_rate(2)
-        product(0, nc.vector)
-        slope(1)
-        scatter(0)
-        deriv(1, nc.gpsimd)
-        product(1, nc.gpsimd)
-        add(0)
-        turn(1, dnew_sb[1], True)
-        slope(2)
-        scatter(1)
-        deriv(2, nc.gpsimd)
-        product(2, nc.gpsimd)
-        add(1)
-        turn(2, dnew_sb[2], True)
-        round_pair("s", 0, slice(0, T))
-        difference(3)
-        scatter(2)
-        slope(3)
-        deriv(3, nc.gpsimd)
-        add(2)
-        grad_rate(3)
-        scatter(3)
 
-        last = PACK - 1
+        gather_grad(1, "hid_w")
+        gather_diff(0)
+        gather_diff(1)
+        term[0] = slot_tile("term", 0)
+        nc.vector.scalar_tensor_tensor(term[0][:], sg[0][:], 1.0, diff[0][:], ALU.subtract, ALU.mult)
+        gather_grad(2)
+        nc.vector.scalar_tensor_tensor(deriv[0][:], term[0][:], 1.0, sg[0][:], ALU.subtract, ALU.mult)
+        gather_diff(2)
+        nc.vector.tensor_tensor(dl[0][:], deriv[0][:], grad_rate[0][:], ALU.mult)
+
+        slope_term(1, "deriv0")
+        scatter(0)
+        finish_on_gpsimd(1)
+        add_on_tensor(0)
+        turn(1, dnew_sb[1], True)
+        slope_term(2, "dl0")
+        scatter(1)
+        finish_on_gpsimd(2)
+        add_on_tensor(1)
+        turn(2, dnew_sb[2], True)
+        round_pair(nc.scalar.copy, 0, slice(0, T))
+
+        gather_diff(LAST, "dl1")
+        scatter(2)
+        term[LAST] = slot_tile("term", LAST)
+        nc.gpsimd.tensor_tensor(term[LAST][:], neg_slope[:], diff[LAST][:], ALU.mult)
+        nc.gpsimd.tensor_tensor(deriv[LAST][:], term[LAST][:], sg[LAST][:], ALU.subtract)
+        add_on_tensor(2)
+        gather_grad(LAST, "dl2")
+        nc.vector.tensor_tensor(df[LAST][:].indirect(places[:]), deriv[LAST][:], grad_rate[LAST][:], ALU.mult)
+
         y_codes = held("y_codes", [P, T], U32)
         y_scales = held("y_scales", [P, T], U8)
-        words_v = out_1[0].rearrange("p n t -> p (n t)").bitcast(I32)
+        words_out = out_1[0].rearrange("p n r -> p (n r)").bitcast(I32)
+        middle = (SCALAR_COLS + T) // 2
+        pieces = (slice(0, SCALAR_COLS), slice(SCALAR_COLS, middle), slice(middle, T))
+        for cols in pieces:
+            nc.vector.tensor_tensor(y[:, LAST, cols], dnew_sb[LAST][:, cols], df[LAST][:, cols], ALU.add)
+            nc.sync.dma_start(out_planes[:, LAST, cols], y[:, LAST, cols])
+        round_pair(nc.scalar.copy, 2, pieces[0])
+        round_pair(nc.vector.tensor_copy, 2, pieces[1])
+        round_pair(nc.vector.tensor_copy, 2, pieces[2])
         for h in range(2):
-            cols = slice(h * BANK, (h + 1) * BANK)
-            add_on_vector(last, h)
-            nc.sync.dma_start(out_v[:, last, cols], y[:, last, cols])
-        round_pair("s", 2, slice(0, BANK))
-        round_pair("v", 2, slice(BANK, T))
-        for h in (1, 0):
-            cols = slice(h * BANK, (h + 1) * BANK)
+            cols = slice(h * (T // 2), (h + 1) * (T // 2))
             nc.vector.quantize_mx(
-                out=y_codes[:, cols].bitcast(FP8X4), scales=y_scales[:, cols],
+                out=y_codes[:, cols].bitcast(FP8X4),
+                scales=y_scales[:, cols],
                 in_=y_bf[:, cols, :].rearrange("p t j -> p (t j)"),
             )
-            nc.sync.dma_start(words_v[:, cols], y_codes[:, cols].bitcast(I32))
-        for q in range(4):
+            nc.sync.dma_start(words_out[:, cols], y_codes[:, cols].bitcast(I32))
+        for q in range(QUADRANTS):
             nc.scalar.dma_start(out_2[0, 4 * q : 4 * q + 4, :].bitcast(I32), y_scales[32 * q : 32 * q + 4, :].bitcast(I32))

from contextlib import ExitStack

import concourse.mybir as mybir
from concourse.masks import make_identity

K, U, I, T, E = 512, 2048, 512, 1024, 512
FLOPS = 2 * K * E * I

F32 = mybir.dt.float32
BF16 = mybir.dt.bfloat16
I32 = mybir.dt.int32
U32 = mybir.dt.uint32
U16 = mybir.dt.uint16
U8 = mybir.dt.uint8
FP8X4 = mybir.dt.float8_e4m3fn_x4
ALU = mybir.AluOpType
ACT = mybir.ActivationFunctionType

P = 128
PACK = 4
LAST = PACK - 1
QUADRANTS = 4
BANK = 512
LIST = 16
SCALAR_COLS = 384


def tile_attend_bstoreblend_pl_kernel(tc, wv, hid_words, hid_scales, store, rate, dnew, offs, offs2, out_0, out_1, out_2):
    nc = tc.nc
    with ExitStack() as ctx:
        keep = ctx.enter_context(tc.tile_pool(name="keep", bufs=1))
        work = ctx.enter_context(tc.tile_pool(name="work", bufs=2))
        psum = ctx.enter_context(tc.psum_pool(name="psum", bufs=1))

        def held(name, shape, dtype, reuse=None):
            return keep.tile(shape, dtype, name=name, tag=reuse or name, align_bytes=64)

        def slot_tile(name, j, reuse=None):
            return held("%s%d" % (name, j), [P, I], F32, reuse)

        places = keep.tile([P, I // LIST], U16, name="places")
        tokens = keep.tile([P, I // LIST], U16, name="tokens")
        wv_sb = held("wv_sb", [P, PACK, E], F32)
        hid_w = held("hid_w", [P, U], I32)
        hid_s = held("hid_s", [P, U], U8)
        rate_col = held("rate_col", [P, PACK], F32)
        store_sb = [held("store%d" % j, [P, T], F32) for j in range(PACK)]
        dnew_sb = [held("dnew%d" % j, [P, T], F32) for j in range(PACK)]
        df = [held("df%d" % j, [P, T], F32) for j in range(PACK)]
        y = held("y", [P, PACK, T], F32)
        ident = held("ident", [P, P], F32)

        store_planes = store.rearrange("(p j) t -> p j t", j=PACK)
        dnew_planes = dnew.rearrange("(p j) t -> p j t", j=PACK)
        out_planes = out_0.rearrange("(p j) t -> p j t", j=PACK)

        nc.gpsimd.memset(hid_s[:].bitcast(I32), 0)
        make_identity(nc, ident[:])

        for q in range(QUADRANTS):
            nc.scalar.dma_start(hid_s[32 * q : 32 * q + 4, :].bitcast(I32), hid_scales[0, 4 * q : 4 * q + 4, :].bitcast(I32))
        nc.sync.dma_start(tokens[:], offs2)
        nc.sync.dma_start(places[:], offs)
        nc.sync.dma_start(rate_col[:], rate.rearrange("o (p c) -> p (o c)", c=PACK))
        nc.sync.dma_start(wv_sb[:], wv.rearrange("(p r) e -> p r e", r=PACK))
        nc.sync.dma_start(dnew_sb[0][:], dnew_planes[:, 0, :])
        nc.sync.dma_start(hid_w[:], hid_words[0].rearrange("p n r -> p (n r)").bitcast(I32))
        nc.sync.dma_start(dnew_sb[1][:], dnew_planes[:, 1, :])
        nc.sync.dma_start(store_sb[0][:], store_planes[:, 0, :])
        nc.sync.dma_start(store_sb[1][:], store_planes[:, 1, :])
        nc.sync.dma_start(dnew_sb[2][:], dnew_planes[:, 2, :])
        nc.sync.dma_start(store_sb[2][:], store_planes[:, 2, :])
        nc.sync.dma_start(store_sb[3][:], store_planes[:, 3, :])
        nc.sync.dma_start(dnew_sb[3][:], dnew_planes[:, 3, :])

        for j in range(PACK):
            (nc.vector if j < PACK // 2 else nc.gpsimd).memset(df[j][:], 0.0)

        centre = held("centre", [P, 1], F32)
        nc.scalar.activation(centre[:], ident[:, 0:1], ACT.Sigmoid, scale=0.0)

        rate_ps = psum.tile([P, PACK, P], F32, name="rate_ps", tag="turn0")
        for c in range(PACK):
            nc.tensor.transpose(rate_ps[:, c, :], rate_col[:, c : c + 1].to_broadcast([P, P]), ident[:])
        rate_sb = held("rate_sb", [P, I], F32)
        nc.scalar.copy(rate_sb[:].rearrange("x (p c) -> x p c", c=PACK), rate_ps[:].rearrange("x c p -> x p c"))

        grad_rate = {}

        def gather_grad(j, reuse=None):
            grad_rate[j] = slot_tile("grad_rate", j, reuse)
            nc.vector.tensor_tensor(grad_rate[j][:], dnew_sb[j][:].indirect(places[:]), rate_sb[:], ALU.mult)

        gather_grad(0)
        hid_s_listed = held("hid_s_listed", [P, I], U8)
        nc.vector.tensor_copy(hid_s_listed[:], hid_s[:].indirect(tokens[:]))

        wv_codes = held("wv_codes", [P, E], U32, "hid_s")
        wv_scales = held("wv_scales", [P, E], U8)
        wv_bf = [held("wv_bf%d" % h, [P, 2, P, PACK], BF16) for h in range(2)]
        wv_dealt = wv_sb[:].rearrange("p r (m j) -> p m j r", j=PACK)
        nc.scalar.copy(wv_bf[0][:].rearrange("p j m r -> p m j r"), wv_dealt[:, :, 0:2, :])
        nc.vector.tensor_copy(wv_bf[1][:].rearrange("p j m r -> p m j r"), wv_dealt[:, :, 2:4, :])
        for h in (1, 0):
            cols = slice(h * (E // 2), (h + 1) * (E // 2))
            nc.vector.quantize_mx(
                out=wv_codes[:, cols].bitcast(FP8X4),
                scales=wv_scales[:, cols],
                in_=wv_bf[h][:].rearrange("p j m r -> p (j m r)"),
            )
        hid_w_listed = held("hid_w_listed", [P, I], U32, "wv_bf0")
        nc.vector.tensor_copy(hid_w_listed[:], hid_w[:].bitcast(U32).indirect(tokens[:]))

        v_sb = [slot_tile("v", j) for j in range(PACK)]
        sg = [slot_tile("sg", j) for j in range(PACK)]
        off_sq = {j: slot_tile("off_sq", j) for j in range(1, PACK)}
        neg_slope = held("neg_slope", [P, I], F32)
        deriv = [slot_tile("deriv", j) for j in range(PACK)]
        dl = [slot_tile("dl", j) for j in range(LAST)]
        diff = {}
        term = {}

        def values(j):
            v_ps = psum.tile([P, I], F32, name="v_ps", tag="v%d" % j)
            cols = slice(j * P, (j + 1) * P)
            nc.tensor.matmul_mx(
                out=v_ps[:],
                lhsT=wv_codes[:, cols].bitcast(FP8X4),
                lhsT_scale=wv_scales[:, cols],
                rhs=hid_w_listed[:].bitcast(FP8X4),
                rhs_scale=hid_s_listed[:],
                start=True,
                stop=True,
            )
            nc.scalar.copy(v_sb[j][:], v_ps[:])

        def gate(j):
            nc.scalar.activation(sg[j][:], store_sb[j][:].indirect(places[:]), ACT.Sigmoid)
            if j in off_sq:
                nc.scalar.activation(off_sq[j][:], sg[j][:], ACT.Square, bias=centre[:], scale=-1.0)

        def gather_diff(j, reuse=None):
            diff[j] = slot_tile("diff", j, reuse)
            nc.vector.tensor_tensor(diff[j][:], store_sb[j][:].indirect(places[:]), v_sb[j][:], ALU.subtract)

        def slope_term(j, reuse):
            term[j] = slot_tile("term", j, reuse)
            nc.vector.scalar_tensor_tensor(term[j][:], off_sq[j][:], 0.25, diff[j][:], ALU.subtract, ALU.mult)

        def finish_on_gpsimd(j):
            nc.gpsimd.tensor_tensor(deriv[j][:], term[j][:], sg[j][:], ALU.subtract)
            nc.gpsimd.tensor_tensor(dl[j][:], deriv[j][:], grad_rate[j][:], ALU.mult)

        def scatter(j):
            nc.vector.tensor_copy(df[j][:].indirect(places[:]), dl[j][:])

        turned = {}

        def turn(j, src, first):
            for h in range(2):
                if first:
                    turned[j, h] = psum.tile([P, BANK], F32, name="turned", tag="turn%d" % (2 * (j % 2) + h))
                for b in range(BANK // P):
                    cols = slice(h * BANK + b * P, h * BANK + (b + 1) * P)
                    nc.tensor.matmul(
                        turned[j, h][:, b * P : (b + 1) * P],
                        src[:, cols],
                        ident[:],
                        start=first and b == 0,
                        stop=(not first) and b == BANK // P - 1,
                        is_transpose=True,
                    )

        def add_on_tensor(j):
            turn(j, df[j], False)
            y_turned = [work.tile([P, BANK], F32, name="y_turned") for h in range(2)]
            for h in range(2):
                nc.scalar.copy(y_turned[h][:], turned[j, h][:])
            for h in range(2):
                back = psum.tile([P, BANK], F32, name="back", tag="turn%d" % (2 * ((j + 1) % 2) + h))
                for b in range(BANK // P):
                    nc.tensor.transpose(back[:, b * P : (b + 1) * P], y_turned[h][:, b * P : (b + 1) * P], ident[:])
                nc.scalar.copy(y[:, j, h * BANK : (h + 1) * BANK], back[:])
            nc.scalar.dma_start(out_planes[:, j, :], y[:, j, :])

        y_bf = held("y_bf", [P, T, PACK], BF16)

        def round_pair(copy, j0, cols):
            copy(y_bf[:, cols, j0 : j0 + 2], y[:, j0 : j0 + 2, cols].rearrange("p j t -> p t j"))

        values(0)
        values(1)
        gate(0)
        values(2)
        gate(1)
        gate(2)
        values(LAST)
        gate(LAST)
        nc.scalar.activation(neg_slope[:], off_sq[LAST][:], ACT.Identity, bias=-0.25)
        turn(0, dnew_sb[0], True)

        gather_grad(1, "hid_w")
        gather_diff(0)
        gather_diff(1)
        term[0] = slot_tile("term", 0)
        nc.vector.scalar_tensor_tensor(term[0][:], sg[0][:], 1.0, diff[0][:], ALU.subtract, ALU.mult)
        gather_grad(2)
        nc.vector.scalar_tensor_tensor(deriv[0][:], term[0][:], 1.0, sg[0][:], ALU.subtract, ALU.mult)
        gather_diff(2)
        nc.vector.tensor_tensor(dl[0][:], deriv[0][:], grad_rate[0][:], ALU.mult)

        slope_term(1, "deriv0")
        scatter(0)
        finish_on_gpsimd(1)
        add_on_tensor(0)
        turn(1, dnew_sb[1], True)
        slope_term(2, "dl0")
        scatter(1)
        finish_on_gpsimd(2)
        add_on_tensor(1)
        turn(2, dnew_sb[2], True)
        round_pair(nc.scalar.copy, 0, slice(0, T))

        gather_diff(LAST, "dl1")
        scatter(2)
        term[LAST] = slot_tile("term", LAST)
        nc.gpsimd.tensor_tensor(term[LAST][:], neg_slope[:], diff[LAST][:], ALU.mult)
        nc.gpsimd.tensor_tensor(deriv[LAST][:], term[LAST][:], sg[LAST][:], ALU.subtract)
        add_on_tensor(2)
        gather_grad(LAST, "dl2")
        nc.vector.tensor_tensor(df[LAST][:].indirect(places[:]), deriv[LAST][:], grad_rate[LAST][:], ALU.mult)

        y_codes = held("y_codes", [P, T], U32)
        y_scales = held("y_scales", [P, T], U8)
        words_out = out_1[0].rearrange("p n r -> p (n r)").bitcast(I32)
        middle = (SCALAR_COLS + T) // 2
        pieces = (slice(0, SCALAR_COLS), slice(SCALAR_COLS, middle), slice(middle, T))
        for cols in pieces:
            nc.vector.tensor_tensor(y[:, LAST, cols], dnew_sb[LAST][:, cols], df[LAST][:, cols], ALU.add)
            nc.sync.dma_start(out_planes[:, LAST, cols], y[:, LAST, cols])
        round_pair(nc.scalar.copy, 2, pieces[0])
        round_pair(nc.vector.tensor_copy, 2, pieces[1])
        round_pair(nc.vector.tensor_copy, 2, pieces[2])
        for h in range(2):
            cols = slice(h * (T // 2), (h + 1) * (T // 2))
            nc.vector.quantize_mx(
                out=y_codes[:, cols].bitcast(FP8X4),
                scales=y_scales[:, cols],
                in_=y_bf[:, cols, :].rearrange("p t j -> p (t j)"),
            )
            nc.sync.dma_start(words_out[:, cols], y_codes[:, cols].bitcast(I32))
        for q in range(QUADRANTS):
            nc.scalar.dma_start(out_2[0, 4 * q : 4 * q + 4, :].bitcast(I32), y_scales[32 * q : 32 * q + 4, :].bitcast(I32))
